import numpy as np, ml_dtypes
CORES = [66,74,82,90,194,202,210,218]
N = 8
import mx_ref
NC, G = 128, 4
C = np.float32(0.00048828125)
BF = ml_dtypes.bfloat16
def cut(t, i, w=512):
    return t[:, w * i:w * i + w]
def tile(rs):
    return np.stack(rs, axis=2).reshape(128, -1).astype(BF)
def layer(w, X):
    out = []
    for i in range(G):
        for t in range(len(X)):
            p = mx_ref.matmul(mx_ref.quantize(cut(w, len(X) * i + t)), X[t])
            z = p if t == 0 else z + p
        out.append(z)
    return out
def gate(U, V):
    return [(np.maximum(u, 0) * v) * C for u, v in zip(U, V)]
def setup_inputs(rng):
    def f(*shape):
        return mx_ref.flush((rng.standard_normal(shape, dtype=np.float32) * np.exp2(rng.integers(-2, 3, shape[:-1] + (1,)))).astype(BF))
    return {"x": f(N, 128, 4 * NC), "u": f(N, 128, G * 512), "v": f(N, 128, G * 512), "w2": f(N, 128, 512)}
def setup_inputs_blocks(rng):
    d = setup_inputs(rng)
    for k in ("x", "u", "v", "w2"): d[k] = mx_ref.spread(d[k], rng, 4)
    return d
def setup_inputs_wide(rng):
    d = setup_inputs(rng)
    for k in ("x", "u", "v", "w2"): d[k] = mx_ref.flush((d[k].astype(np.float32) * np.exp2(rng.integers(-5, 6, (N, 1, 1))).astype(np.float32)).astype(BF))
    return d
def setup_inputs_zeros(rng):
    d = setup_inputs(rng); v = d["x"].reshape(N, 128, -1, 4).copy()
    v[np.broadcast_to((rng.random((N, 1, v.shape[2], 1)) < 0.33), v.shape)] = 0
    d["x"] = v.reshape(d["x"].shape)
    return d
def reference(x, u, v, w2):
    h = np.zeros((N, 128, 4 * NC), BF)
    for j in range(N):
        X = [mx_ref.quantize(x[j])]
        h[j] = tile(gate(layer(u[j], X), layer(v[j], X)))
    H = [mx_ref.quantize(h[j]) for j in range(N)]
    y = np.zeros((N, 128, N * NC), np.float32)
    for r in range(N):
        qw = mx_ref.quantize(w2[r])
        for j in range(N):
            y[r][:, NC * j:NC * j + NC] = mx_ref.matmul(qw, H[j])
    return {"y": y}

@@ -1,0 +1,166 @@
+from concourse.bass import DstId, RemoteDMATransfer
+from concourse.mybir import dt, AluOpType, ActivationFunctionType
+
+N = 8
+NC = 128
+G = 4
+C = 0.00048828125
+
+SCRATCH = {
+    "xb": ("sbuf", [128, 4 * NC], "bfloat16"),
+    "ub": ("sbuf", [128, G * 512], "bfloat16"),
+    "vb": ("sbuf", [128, G * 512], "bfloat16"),
+    "wb": ("sbuf", [128, 512], "bfloat16"),
+    "xq": ("sbuf", [128, NC], "float8_e4m3fn_x4"),
+    "xs": ("sbuf", [128, NC], "uint8"),
+    "uq": ("sbuf", [128, G * 128], "float8_e4m3fn_x4"),
+    "us": ("sbuf", [128, G * 128], "uint8"),
+    "vq": ("sbuf", [128, G * 128], "float8_e4m3fn_x4"),
+    "vs": ("sbuf", [128, G * 128], "uint8"),
+    "wq": ("sbuf", [128, 128], "float8_e4m3fn_x4"),
+    "ws": ("sbuf", [128, 128], "uint8"),
+    "rl": ("sbuf", [128, G * NC], "float32"),
+    "hb": ("sbuf", [128, 4 * NC], "bfloat16"),
+    "hq": ("sbuf", [128, N * NC], "float8_e4m3fn_x4"),
+    "hs": ("sbuf", [128, N * NC], "uint8"),
+    "yb": ("sbuf", [128, N * NC], "float32"),
+    "ps": ("psum", [128, 8 * 512], "float32"),
+}
+SEMAPHORES = (
+    ["ld_x", "ld_u", "ld_va", "ld_vb", "ld_w", "q_x", "q_u", "q_w", "q_h", "ml", "mt", "ls", "st"]
+    + ["q_v%d" % b for b in range(G)] + ["m_u%d" % b for b in range(G)] + ["m_v%d" % b for b in range(G)]
+    + ["r_%d" % b for b in range(G)] + ["pl%d" % k for k in range(N // 2)] + ["cp%d" % k for k in range(N // 2)]
+    + ["my%d" % j for j in range(N)]
+)
+
+
+def rank_program(g, core, T, topo):
+    rank = T.rank_of(core)
+    if rank is None:
+        return
+    S = T.sem
+    cores = list(T.cores)
+
+    def mate_of(c):
+        return [d for d in cores if topo.mates(c, d)][0]
+
+    pairs = []
+    for c in cores:
+        if not any(c in p for p in pairs):
+            pairs.append((c, mate_of(c)))
+    pair_of = {c: k for k, p in enumerate(pairs) for c in p}
+    slot_of = {c: 2 * k + i for k, p in enumerate(pairs) for i, c in enumerate(p)}
+    mate = mate_of(core)
+    plane = [d for d in cores if d == core or topo.same_plane(core, d)]
+    me = plane.index(core)
+    send_to = [plane[(me + s) % len(plane)] for s in range(1, len(plane))]
+    take_from = [plane[(me - s) % len(plane)] for s in range(1, len(plane))]
+    kp = pair_of[core]
+
+    def codes(a, b):
+        return T.hq[:, a:b].bitcast(dt.uint8)
+
+    def bank(j, n=NC):
+        return T.ps[:, 512 * j:512 * j + n]
+
+    g.scalar.dma_start(T.ub[:], T.u[:]).then_inc(S.ld_u, 16)
+    g.sync.dma_start(T.xb[:], T.x[:]).then_inc(S.ld_x, 16)
+    cutv = (G - 1) * 512
+    g.sync.dma_start(T.vb[:, 0:cutv], T.v[:, 0:cutv]).then_inc(S.ld_va, 16)
+    g.sync.dma_start(T.vb[:, cutv:], T.v[:, cutv:]).then_inc(S.ld_vb, 16)
+    g.sync.dma_start(T.wb[:], T.w2[:]).then_inc(S.ld_w, 16)
+
+    V, P, A = g.vector, g.tensor, g.scalar
+
+    def quant_v(b):
+        V.quantize_mx(T.vq[:, 128 * b:128 * b + 128], T.vs[:, 128 * b:128 * b + 128],
+                      T.vb[:, 512 * b:512 * b + 512]).then_inc(S["q_v%d" % b], 1)
+
+    def gate(b):
+        V.wait_ge(S["r_%d" % b], 1)
+        V.wait_ge(S["m_v%d" % b], 1)
+        V.tensor_tensor(T.hb[:, b:4 * NC:4], T.rl[:, NC * b:NC * b + NC], bank(G + b), AluOpType.mult).then_inc(S.ml, 1)
+
+    V.wait_ge(S.ld_x, 16)
+    V.quantize_mx(T.xq[:], T.xs[:], T.xb[:]).then_inc(S.q_x, 1)
+    V.wait_ge(S.ld_u, 16)
+    V.quantize_mx(T.uq[:], T.us[:], T.ub[:]).then_inc(S.q_u, 1)
+    V.wait_ge(S.ld_va, 16)
+    for b in range(G - 1):
+        quant_v(b)
+    for b in range(G - 1):
+        gate(b)
+    V.wait_ge(S.ld_vb, 16)
+    quant_v(G - 1)
+    gate(G - 1)
+    a0 = NC * slot_of[core]
+    V.wait_ge(S.ml, G)
+    V.quantize_mx(T.hq[:, a0:a0 + NC], T.hs[:, a0:a0 + NC], T.hb[:]).then_inc(S.q_h, 1)
+    V.wait_ge(S.ld_w, 16)
+    V.quantize_mx(T.wq[:], T.ws[:], T.wb[:]).then_inc(S.q_w, 1)
+
+    P.wait_ge(S.q_x, 1)
+    P.wait_ge(S.q_u, 1)
+    for b in range(G):
+        P.matmul_mx(bank(b), T.uq[:, 128 * b:128 * b + 128], T.us[:, 128 * b:128 * b + 128],
+                    T.xq[:], T.xs[:], True, True).then_inc(S["m_u%d" % b], 1)
+    for b in range(G):
+        P.wait_ge(S["q_v%d" % b], 1)
+        P.matmul_mx(bank(G + b), T.vq[:, 128 * b:128 * b + 128], T.vs[:, 128 * b:128 * b + 128],
+                    T.xq[:], T.xs[:], True, True).then_inc(S["m_v%d" % b], 1)
+
+    for b in range(G):
+        A.wait_ge(S["m_u%d" % b], 1)
+        A.activation(T.rl[:, NC * b:NC * b + NC], bank(b), ActivationFunctionType.Relu, scale=C).then_inc(S["r_%d" % b], 1)
+
+    sent = 0
+    rid, pid = topo.addr(mate, core)
+    mk = topo.mask(core, mate)
+    ne_m = bin(mk).count("1")
+    g.wait_ge(S.q_h, 1)
+    g.remote_dma(T.hs[:, a0:a0 + NC], T.hs[:, a0:a0 + NC], S.mt, S.ls, pid, rid, mk)
+    g.remote_dma(codes(a0, a0 + NC), codes(a0, a0 + NC), S.mt, S.ls, pid, rid, mk)
+    sent += 2 * ne_m
+
+    p0 = 2 * NC * kp
+    mk = topo.mask(core, send_to[0])
+    for d in send_to:
+        mk &= topo.mask(core, d)
+    ne_p = bin(mk).count("1")
+    ids = [DstId(rid=topo.addr(d, core)[0], pnc=topo.addr(d, core)[1]) for d in send_to]
+    g.wait_ge(S.mt, 2 * ne_m)
+    for view in (T.hs[:, p0:p0 + 2 * NC], codes(p0, p0 + 2 * NC)):
+        g.remote_dma_fused([RemoteDMATransfer(dst_ids=ids, dma_engine_mask=mk, remote_sem=S["pl%d" % kp],
+                                              srcs=[view], dsts=[view for d in send_to])], local_sem=S.ls)
+        sent += ne_p
+
+    P.wait_ge(S.q_w, 1)
+    P.wait_ge(S.q_h, 1)
+    stores = 0
+    for k in [kp] + [pair_of[d] for d in take_from]:
+        if k == kp:
+            P.wait_ge(S.mt, 2 * ne_m)
+        else:
+            P.wait_ge(S["pl%d" % k], 2 * ne_p)
+        for i in range(2):
+            j = 2 * k + i
+            P.matmul_mx(bank(j), T.wq[:], T.ws[:], T.hq[:, NC * j:NC * j + NC], T.hs[:, NC * j:NC * j + NC],
+                        True, True).then_inc(S["my%d" % j], 1)
+        j = 2 * k
+        V.wait_ge(S["my%d" % j], 1)
+        V.tensor_copy(T.yb[:, NC * j:NC * j + NC], bank(j)).then_inc(S["cp%d" % k], 1)
+        j = 2 * k + 1
+        A.wait_ge(S["my%d" % j], 1)
+        A.activation(T.yb[:, NC * j:NC * j + NC], bank(j), ActivationFunctionType.Copy).then_inc(S["cp%d" % k], 1)
+        g.sync.wait_ge(S["cp%d" % k], 2)
+        r0, r1 = T.rank_of(pairs[k][0]), T.rank_of(pairs[k][1])
+        j = 2 * k
+        if r1 == r0 + 1:
+            g.sync.dma_start(T.y[:, NC * r0:NC * r0 + 2 * NC], T.yb[:, NC * j:NC * j + 2 * NC]).then_inc(S.st, 16)
+            stores += 1
+        else:
+            for i, r in enumerate((r0, r1)):
+                g.sync.dma_start(T.y[:, NC * r:NC * r + NC], T.yb[:, NC * (j + i):NC * (j + i) + NC]).then_inc(S.st, 16)
+                stores += 1
+    g.sync.wait_ge(S.st, 16 * stores)
+    g.wait_ge(S.ls, sent)

@@ -26,11 +26,15 @@ SCRATCH = {
     "yb": ("sbuf", [128, N * NC], "float32"),
     "ps": ("psum", [128, 8 * 512], "float32"),
 }
+PIECES_U = [(0, 2), (2, 4)]
+PIECES_V = [(0, 2), (2, 3), (3, 4)]
 SEMAPHORES = (
-    ["ld_x", "ld_u", "ld_va", "ld_vb", "ld_w", "q_x", "q_u", "q_w", "q_h", "ml", "mt", "ls", "st"]
-    + ["q_v%d" % b for b in range(G)] + ["m_u%d" % b for b in range(G)] + ["m_v%d" % b for b in range(G)]
-    + ["r_%d" % b for b in range(G)] + ["pl%d" % k for k in range(N // 2)] + ["cp%d" % k for k in range(N // 2)]
-    + ["my%d" % j for j in range(N)]
+    ["ld_x", "ld_w", "q_x", "q_w", "q_h", "ml", "ls", "st"]
+    + ["ld_u%d" % i for i in range(len(PIECES_U))] + ["ld_v%d" % i for i in range(len(PIECES_V))]
+    + ["q_u%d" % i for i in range(len(PIECES_U))] + ["q_v%d" % i for i in range(len(PIECES_V))]
+    + ["m_u%d" % b for b in range(G)] + ["m_v%d" % b for b in range(G)] + ["r_%d" % b for b in range(G)]
+    + ["s%d" % j for j in range(N)] + ["c%d" % j for j in range(N)] + ["sp%d" % k for k in range(N // 2)]
+    + ["cp%d" % j for j in range(N)] + ["my%d" % j for j in range(N)]
 )
 
 
@@ -40,6 +44,7 @@ def rank_program(g, core, T, topo):
         return
     S = T.sem
     cores = list(T.cores)
+    V, P, A = g.vector, g.tensor, g.scalar
 
     def mate_of(c):
         return [d for d in cores if topo.mates(c, d)][0]
@@ -50,31 +55,34 @@ def rank_program(g, core, T, topo):
             pairs.append((c, mate_of(c)))
     pair_of = {c: k for k, p in enumerate(pairs) for c in p}
     slot_of = {c: 2 * k + i for k, p in enumerate(pairs) for i, c in enumerate(p)}
+    rank_at = {slot_of[c]: T.rank_of(c) for c in cores}
     mate = mate_of(core)
     plane = [d for d in cores if d == core or topo.same_plane(core, d)]
     me = plane.index(core)
     send_to = [plane[(me + s) % len(plane)] for s in range(1, len(plane))]
     take_from = [plane[(me - s) % len(plane)] for s in range(1, len(plane))]
-    kp = pair_of[core]
+    kp, sl, sm = pair_of[core], slot_of[core], slot_of[mate]
 
-    def codes(a, b):
-        return T.hq[:, a:b].bitcast(dt.uint8)
+    def codes(j, n=1):
+        return T.hq[:, NC * j:NC * (j + n)].bitcast(dt.uint8)
 
-    def bank(j, n=NC):
-        return T.ps[:, 512 * j:512 * j + n]
+    def planes(j, n=1):
+        return T.hs[:, NC * j:NC * (j + n)]
 
-    g.scalar.dma_start(T.ub[:], T.u[:]).then_inc(S.ld_u, 16)
-    g.sync.dma_start(T.xb[:], T.x[:]).then_inc(S.ld_x, 16)
-    cutv = (G - 1) * 512
-    g.sync.dma_start(T.vb[:, 0:cutv], T.v[:, 0:cutv]).then_inc(S.ld_va, 16)
-    g.sync.dma_start(T.vb[:, cutv:], T.v[:, cutv:]).then_inc(S.ld_vb, 16)
+    def bank(j):
+        return T.ps[:, 512 * j:512 * j + NC]
+
+    A.dma_start(T.xb[:], T.x[:]).then_inc(S.ld_x, 16)
+    for i, (a, b) in enumerate(PIECES_U):
+        g.sync.dma_start(T.ub[:, 512 * a:512 * b], T.u[:, 512 * a:512 * b]).then_inc(S["ld_u%d" % i], 16)
+    for i, (a, b) in enumerate(PIECES_V):
+        g.sync.dma_start(T.vb[:, 512 * a:512 * b], T.v[:, 512 * a:512 * b]).then_inc(S["ld_v%d" % i], 16)
     g.sync.dma_start(T.wb[:], T.w2[:]).then_inc(S.ld_w, 16)
 
-    V, P, A = g.vector, g.tensor, g.scalar
-
-    def quant_v(b):
-        V.quantize_mx(T.vq[:, 128 * b:128 * b + 128], T.vs[:, 128 * b:128 * b + 128],
-                      T.vb[:, 512 * b:512 * b + 512]).then_inc(S["q_v%d" % b], 1)
+    def quant(name, i, a, b):
+        V.wait_ge(S["ld_%s%d" % (name, i)], 16)
+        V.quantize_mx(T[name + "q"][:, 128 * a:128 * b], T[name + "s"][:, 128 * a:128 * b],
+                      T[name + "b"][:, 512 * a:512 * b]).then_inc(S["q_%s%d" % (name, i)], 1)
 
     def gate(b):
         V.wait_ge(S["r_%d" % b], 1)
@@ -83,84 +91,91 @@ def rank_program(g, core, T, topo):
 
     V.wait_ge(S.ld_x, 16)
     V.quantize_mx(T.xq[:], T.xs[:], T.xb[:]).then_inc(S.q_x, 1)
-    V.wait_ge(S.ld_u, 16)
-    V.quantize_mx(T.uq[:], T.us[:], T.ub[:]).then_inc(S.q_u, 1)
-    V.wait_ge(S.ld_va, 16)
-    for b in range(G - 1):
-        quant_v(b)
-    for b in range(G - 1):
-        gate(b)
-    V.wait_ge(S.ld_vb, 16)
-    quant_v(G - 1)
-    gate(G - 1)
-    a0 = NC * slot_of[core]
+    for i, (a, b) in enumerate(PIECES_U):
+        quant("u", i, a, b)
+    due = []
+    for i, (a, b) in enumerate(PIECES_V):
+        quant("v", i, a, b)
+        for t in due:
+            gate(t)
+        due = list(range(a, b))
+    for t in due:
+        gate(t)
     V.wait_ge(S.ml, G)
-    V.quantize_mx(T.hq[:, a0:a0 + NC], T.hs[:, a0:a0 + NC], T.hb[:]).then_inc(S.q_h, 1)
+    V.quantize_mx(T.hq[:, NC * sl:NC * sl + NC], planes(sl), T.hb[:]).then_inc(S.q_h, 1)
     V.wait_ge(S.ld_w, 16)
     V.quantize_mx(T.wq[:], T.ws[:], T.wb[:]).then_inc(S.q_w, 1)
 
     P.wait_ge(S.q_x, 1)
-    P.wait_ge(S.q_u, 1)
-    for b in range(G):
-        P.matmul_mx(bank(b), T.uq[:, 128 * b:128 * b + 128], T.us[:, 128 * b:128 * b + 128],
-                    T.xq[:], T.xs[:], True, True).then_inc(S["m_u%d" % b], 1)
-    for b in range(G):
-        P.wait_ge(S["q_v%d" % b], 1)
-        P.matmul_mx(bank(G + b), T.vq[:, 128 * b:128 * b + 128], T.vs[:, 128 * b:128 * b + 128],
-                    T.xq[:], T.xs[:], True, True).then_inc(S["m_v%d" % b], 1)
+    for name, pieces, first in (("u", PIECES_U, 0), ("v", PIECES_V, G)):
+        for i, (a, b) in enumerate(pieces):
+            P.wait_ge(S["q_%s%d" % (name, i)], 1)
+            for t in range(a, b):
+                P.matmul_mx(bank(first + t), T[name + "q"][:, 128 * t:128 * t + 128], T[name + "s"][:, 128 * t:128 * t + 128],
+                            T.xq[:], T.xs[:], True, True).then_inc(S["m_%s%d" % (name, t)], 1)
 
     for b in range(G):
         A.wait_ge(S["m_u%d" % b], 1)
         A.activation(T.rl[:, NC * b:NC * b + NC], bank(b), ActivationFunctionType.Relu, scale=C).then_inc(S["r_%d" % b], 1)
 
-    sent = 0
-    rid, pid = topo.addr(mate, core)
     mk = topo.mask(core, mate)
-    ne_m = bin(mk).count("1")
-    g.wait_ge(S.q_h, 1)
-    g.remote_dma(T.hs[:, a0:a0 + NC], T.hs[:, a0:a0 + NC], S.mt, S.ls, pid, rid, mk)
-    g.remote_dma(codes(a0, a0 + NC), codes(a0, a0 + NC), S.mt, S.ls, pid, rid, mk)
-    sent += 2 * ne_m
-
-    p0 = 2 * NC * kp
-    mk = topo.mask(core, send_to[0])
     for d in send_to:
         mk &= topo.mask(core, d)
-    ne_p = bin(mk).count("1")
-    ids = [DstId(rid=topo.addr(d, core)[0], pnc=topo.addr(d, core)[1]) for d in send_to]
-    g.wait_ge(S.mt, 2 * ne_m)
-    for view in (T.hs[:, p0:p0 + 2 * NC], codes(p0, p0 + 2 * NC)):
-        g.remote_dma_fused([RemoteDMATransfer(dst_ids=ids, dma_engine_mask=mk, remote_sem=S["pl%d" % kp],
-                                              srcs=[view], dsts=[view for d in send_to])], local_sem=S.ls)
-        sent += ne_p
+    ne = bin(mk).count("1")
+    sent = [0]
 
+    def send(view, dests, sem):
+        ids = [DstId(rid=topo.addr(d, core)[0], pnc=topo.addr(d, core)[1]) for d in dests]
+        g.remote_dma_fused([RemoteDMATransfer(dst_ids=ids, dma_engine_mask=mk, remote_sem=sem,
+                                              srcs=[view], dsts=[view for d in dests])], local_sem=S.ls)
+        sent[0] += ne
+
+    g.wait_ge(S.q_h, 1)
+    send(planes(sl), [mate], S["s%d" % sl])
+    send(codes(sl), [mate] + send_to, S["c%d" % sl])
+    g.wait_ge(S["s%d" % sm], ne)
+    send(planes(2 * kp, 2), send_to, S["sp%d" % kp])
+    g.wait_ge(S["c%d" % sm], ne)
+    send(codes(sm), send_to, S["c%d" % sm])
+
+    near = [slot_of[d] for d in take_from]
+    far = [slot_of[mate_of(d)] for d in take_from]
     P.wait_ge(S.q_w, 1)
     P.wait_ge(S.q_h, 1)
-    stores = 0
-    for k in [kp] + [pair_of[d] for d in take_from]:
-        if k == kp:
-            P.wait_ge(S.mt, 2 * ne_m)
+    for n, j in enumerate([sl, sm] + near + far):
+        if j == sm:
+            P.wait_ge(S["s%d" % j], ne)
+        elif j in near:
+            P.wait_ge(S["sp%d" % (j // 2)], ne)
+        if j != sl:
+            P.wait_ge(S["c%d" % j], ne)
+        P.matmul_mx(bank(j), T.wq[:], T.ws[:], T.hq[:, NC * j:NC * j + NC], planes(j), True, True).then_inc(S["my%d" % j], 1)
+        if n % 2 == 0:
+            V.wait_ge(S["my%d" % j], 1)
+            V.tensor_copy(T.yb[:, NC * j:NC * j + NC], bank(j)).then_inc(S["cp%d" % j], 1)
         else:
-            P.wait_ge(S["pl%d" % k], 2 * ne_p)
-        for i in range(2):
-            j = 2 * k + i
-            P.matmul_mx(bank(j), T.wq[:], T.ws[:], T.hq[:, NC * j:NC * j + NC], T.hs[:, NC * j:NC * j + NC],
-                        True, True).then_inc(S["my%d" % j], 1)
-        j = 2 * k
-        V.wait_ge(S["my%d" % j], 1)
-        V.tensor_copy(T.yb[:, NC * j:NC * j + NC], bank(j)).then_inc(S["cp%d" % k], 1)
-        j = 2 * k + 1
-        A.wait_ge(S["my%d" % j], 1)
-        A.activation(T.yb[:, NC * j:NC * j + NC], bank(j), ActivationFunctionType.Copy).then_inc(S["cp%d" % k], 1)
-        g.sync.wait_ge(S["cp%d" % k], 2)
-        r0, r1 = T.rank_of(pairs[k][0]), T.rank_of(pairs[k][1])
-        j = 2 * k
-        if r1 == r0 + 1:
-            g.sync.dma_start(T.y[:, NC * r0:NC * r0 + 2 * NC], T.yb[:, NC * j:NC * j + 2 * NC]).then_inc(S.st, 16)
-            stores += 1
+            A.wait_ge(S["my%d" % j], 1)
+            A.activation(T.yb[:, NC * j:NC * j + NC], bank(j), ActivationFunctionType.Copy).then_inc(S["cp%d" % j], 1)
+
+    stores = [0]
+
+    def store(js):
+        for j in js:
+            g.sync.wait_ge(S["cp%d" % j], 1)
+        js = sorted(js)
+        if len(js) == 2 and js[1] == js[0] + 1 and rank_at[js[1]] == rank_at[js[0]] + 1:
+            runs = [(js[0], 2)]
         else:
-            for i, r in enumerate((r0, r1)):
-                g.sync.dma_start(T.y[:, NC * r:NC * r + NC], T.yb[:, NC * (j + i):NC * (j + i) + NC]).then_inc(S.st, 16)
-                stores += 1
-    g.sync.wait_ge(S.st, 16 * stores)
-    g.wait_ge(S.ls, sent)
+            runs = [(j, 1) for j in js]
+        for j, w in runs:
+            r = rank_at[j]
+            g.sync.dma_start(T.y[:, NC * r:NC * (r + w)], T.yb[:, NC * j:NC * (j + w)]).then_inc(S.st, 16)
+            stores[0] += 1
+
+    store([sl, sm])
+    store([near[-1]])
+    for a, b in zip(near[:-1], far[:-1]):
+        store([a, b])
+    store([far[-1]])
+    g.sync.wait_ge(S.st, 16 * stores[0])
+    g.wait_ge(S.ls, sent[0])

@@ -2,6 +2,7 @@ from concourse.bass import DstId, RemoteDMATransfer
 from concourse.mybir import dt, AluOpType, ActivationFunctionType
 
 N = 8
+WORLD = 256
 NC = 128
 G = 4
 C = 0.00048828125
@@ -29,45 +30,79 @@ SCRATCH = {
 PIECES_U = [(0, 2), (2, 4)]
 PIECES_V = [(0, 2), (2, 3), (3, 4)]
 SEMAPHORES = (
-    ["ld_x", "ld_w", "q_x", "q_w", "q_h", "ml", "ls", "st"]
+    ["ld_x", "ld_w", "q_x", "q_w", "q_h", "ml", "ls", "st", "sm", "cm", "fc", "ra", "rb"]
     + ["ld_u%d" % i for i in range(len(PIECES_U))] + ["ld_v%d" % i for i in range(len(PIECES_V))]
     + ["q_u%d" % i for i in range(len(PIECES_U))] + ["q_v%d" % i for i in range(len(PIECES_V))]
     + ["m_u%d" % b for b in range(G)] + ["m_v%d" % b for b in range(G)] + ["r_%d" % b for b in range(G)]
-    + ["s%d" % j for j in range(N)] + ["c%d" % j for j in range(N)] + ["sp%d" % k for k in range(N // 2)]
+    + ["c%d" % j for j in range(N)] + ["sp%d" % j for j in range(N)]
     + ["cp%d" % j for j in range(N)] + ["my%d" % j for j in range(N)]
 )
 
 
 def rank_program(g, core, T, topo):
-    rank = T.rank_of(core)
-    if rank is None:
-        return
     S = T.sem
     cores = list(T.cores)
-    V, P, A = g.vector, g.tensor, g.scalar
 
     def mate_of(c):
         return [d for d in cores if topo.mates(c, d)][0]
 
-    pairs = []
-    for c in cores:
-        if not any(c in p for p in pairs):
-            pairs.append((c, mate_of(c)))
-    pair_of = {c: k for k, p in enumerate(pairs) for c in p}
-    slot_of = {c: 2 * k + i for k, p in enumerate(pairs) for i, c in enumerate(p)}
-    rank_at = {slot_of[c]: T.rank_of(c) for c in cores}
-    mate = mate_of(core)
-    plane = [d for d in cores if d == core or topo.same_plane(core, d)]
-    me = plane.index(core)
-    send_to = [plane[(me + s) % len(plane)] for s in range(1, len(plane))]
-    take_from = [plane[(me - s) % len(plane)] for s in range(1, len(plane))]
-    kp, sl, sm = pair_of[core], slot_of[core], slot_of[mate]
+    def ring(c):
+        plane = [d for d in cores if d == c or topo.same_plane(c, d)]
+        me = plane.index(c)
+        to = [plane[(me + s) % len(plane)] for s in range(1, len(plane))]
+        frm = [plane[(me - s) % len(plane)] for s in range(1, len(plane))]
+        return to, frm
+
+    def last_far(c):
+        return mate_of(ring(c)[0][-1])
+
+    def passer_of(c):
+        return [d for d in range(WORLD) if topo.host(d) == topo.host(c) and topo.chip(d) == topo.chip(c)
+                and d not in cores and topo.die(d) != topo.die(c) and topo.may_write(d, last_far(c))][0]
+
+    def masks(c):
+        off = topo.mask(c, mate_of(c))
+        for d in ring(c)[0]:
+            off &= topo.mask(c, d)
+        return off, topo.mask(c, passer_of(c)) & ~off
+
+    def count(m):
+        return bin(m).count("1")
 
     def codes(j, n=1):
         return T.hq[:, NC * j:NC * (j + n)].bitcast(dt.uint8)
 
     def planes(j, n=1):
         return T.hs[:, NC * j:NC * (j + n)]
+
+    sent = [0]
+
+    def send(src, dests, views, sem, mask):
+        ids = [DstId(rid=topo.addr(d, core)[0], pnc=topo.addr(d, core)[1]) for d in dests]
+        g.remote_dma_fused([RemoteDMATransfer(dst_ids=ids, dma_engine_mask=mask, remote_sem=sem,
+                                              srcs=[src], dsts=views)], local_sem=S.ls)
+        sent[0] += count(mask)
+
+    OWN, MATE, NEAR, FAR = 0, 1, 2, 5
+
+    rank = T.rank_of(core)
+    if rank is None:
+        for c in cores:
+            if passer_of(c) == core:
+                g.wait_ge(S.fc, count(masks(c)[1]))
+                send(codes(OWN), [last_far(c)], [codes(FAR + 2)], S.cm, topo.mask(core, last_far(c)))
+                g.wait_ge(S.ls, sent[0])
+        return
+
+    V, P, A = g.vector, g.tensor, g.scalar
+    mate = mate_of(core)
+    send_to, near = ring(core)
+    far = [mate_of(d) for d in near]
+    passer = passer_of(core)
+    off, on = masks(core)
+    ne = count(off)
+    npass = count(topo.mask(passer_of(far[2]), core))
+    R = T.rank_of
 
     def bank(j):
         return T.ps[:, 512 * j:512 * j + NC]
@@ -102,7 +137,7 @@ def rank_program(g, core, T, topo):
     for t in due:
         gate(t)
     V.wait_ge(S.ml, G)
-    V.quantize_mx(T.hq[:, NC * sl:NC * sl + NC], planes(sl), T.hb[:]).then_inc(S.q_h, 1)
+    V.quantize_mx(T.hq[:, NC * OWN:NC * OWN + NC], planes(0), T.hb[:]).then_inc(S.q_h, 1)
     V.wait_ge(S.ld_w, 16)
     V.quantize_mx(T.wq[:], T.ws[:], T.wb[:]).then_inc(S.q_w, 1)
 
@@ -118,64 +153,55 @@ def rank_program(g, core, T, topo):
         A.wait_ge(S["m_u%d" % b], 1)
         A.activation(T.rl[:, NC * b:NC * b + NC], bank(b), ActivationFunctionType.Relu, scale=C).then_inc(S["r_%d" % b], 1)
 
-    mk = topo.mask(core, mate)
-    for d in send_to:
-        mk &= topo.mask(core, d)
-    ne = bin(mk).count("1")
-    sent = [0]
-
-    def send(view, dests, sem):
-        ids = [DstId(rid=topo.addr(d, core)[0], pnc=topo.addr(d, core)[1]) for d in dests]
-        g.remote_dma_fused([RemoteDMATransfer(dst_ids=ids, dma_engine_mask=mk, remote_sem=sem,
-                                              srcs=[view], dsts=[view for d in dests])], local_sem=S.ls)
-        sent[0] += ne
-
+    ks = range(len(send_to))
     g.wait_ge(S.q_h, 1)
-    send(planes(sl), [mate], S["s%d" % sl])
-    send(codes(sl), [mate] + send_to, S["c%d" % sl])
-    g.wait_ge(S["s%d" % sm], ne)
-    send(planes(2 * kp, 2), send_to, S["sp%d" % kp])
-    g.wait_ge(S["c%d" % sm], ne)
-    send(codes(sm), send_to, S["c%d" % sm])
+    send(planes(0), [mate], [planes(1)], S.sm, off)
+    send(codes(OWN), send_to + [mate], [codes(NEAR + k) for k in ks] + [codes(MATE)], S["c%d" % rank], off)
+    send(codes(OWN), [passer], [codes(OWN)], S.fc, on)
+    g.wait_ge(S.sm, ne)
+    send(planes(0, 2), send_to, [planes(2 + 2 * k, 2) for k in ks], S["sp%d" % rank], off)
+    g.wait_ge(S["c%d" % R(near[0])], ne)
+    send(codes(NEAR), [mate], [codes(FAR)], S.ra, off)
+    g.wait_ge(S["c%d" % R(near[1])], ne)
+    send(codes(NEAR + 1), [mate], [codes(FAR + 1)], S.rb, off)
 
-    near = [slot_of[d] for d in take_from]
-    far = [slot_of[mate_of(d)] for d in take_from]
+    todo = [(core, OWN, 0, []), (mate, MATE, 1, [(S.sm, ne), (S["c%d" % R(mate)], ne)])]
+    for k, d in enumerate(near):
+        todo.append((d, NEAR + k, 2 + 2 * k, [(S["sp%d" % R(d)], ne), (S["c%d" % R(d)], ne)]))
+    todo.append((far[0], FAR, 3, [(S.ra, ne)]))
+    todo.append((far[1], FAR + 1, 5, [(S.rb, ne)]))
+    todo.append((far[2], FAR + 2, 7, [(S.cm, npass)]))
     P.wait_ge(S.q_w, 1)
     P.wait_ge(S.q_h, 1)
-    for n, j in enumerate([sl, sm] + near + far):
-        if j == sm:
-            P.wait_ge(S["s%d" % j], ne)
-        elif j in near:
-            P.wait_ge(S["sp%d" % (j // 2)], ne)
-        if j != sl:
-            P.wait_ge(S["c%d" % j], ne)
-        P.matmul_mx(bank(j), T.wq[:], T.ws[:], T.hq[:, NC * j:NC * j + NC], planes(j), True, True).then_inc(S["my%d" % j], 1)
+    for n, (d, cj, pj, waits) in enumerate(todo):
+        r = R(d)
+        for sem, val in waits:
+            P.wait_ge(sem, val)
+        P.matmul_mx(bank(cj), T.wq[:], T.ws[:], T.hq[:, NC * cj:NC * cj + NC], planes(pj), True, True).then_inc(S["my%d" % r], 1)
         if n % 2 == 0:
-            V.wait_ge(S["my%d" % j], 1)
-            V.tensor_copy(T.yb[:, NC * j:NC * j + NC], bank(j)).then_inc(S["cp%d" % j], 1)
+            V.wait_ge(S["my%d" % r], 1)
+            V.tensor_copy(T.yb[:, NC * r:NC * r + NC], bank(cj)).then_inc(S["cp%d" % r], 1)
         else:
-            A.wait_ge(S["my%d" % j], 1)
-            A.activation(T.yb[:, NC * j:NC * j + NC], bank(j), ActivationFunctionType.Copy).then_inc(S["cp%d" % j], 1)
+            A.wait_ge(S["my%d" % r], 1)
+            A.activation(T.yb[:, NC * r:NC * r + NC], bank(cj), ActivationFunctionType.Copy).then_inc(S["cp%d" % r], 1)
 
     stores = [0]
 
-    def store(js):
-        for j in js:
-            g.sync.wait_ge(S["cp%d" % j], 1)
-        js = sorted(js)
-        if len(js) == 2 and js[1] == js[0] + 1 and rank_at[js[1]] == rank_at[js[0]] + 1:
-            runs = [(js[0], 2)]
-        else:
-            runs = [(j, 1) for j in js]
-        for j, w in runs:
-            r = rank_at[j]
-            g.sync.dma_start(T.y[:, NC * r:NC * (r + w)], T.yb[:, NC * j:NC * (j + w)]).then_inc(S.st, 16)
+    def store(ds):
+        rs = sorted(R(d) for d in ds)
+        for r in rs:
+            g.sync.wait_ge(S["cp%d" % r], 1)
+        runs = [(rs[0], 2)] if len(rs) == 2 and rs[1] == rs[0] + 1 else [(r, 1) for r in rs]
+        for r, w in runs:
+            g.sync.dma_start(T.y[:, NC * r:NC * (r + w)], T.yb[:, NC * r:NC * (r + w)]).then_inc(S.st, 16)
             stores[0] += 1
 
-    store([sl, sm])
-    store([near[-1]])
-    for a, b in zip(near[:-1], far[:-1]):
-        store([a, b])
-    store([far[-1]])
+    store([core])
+    store([mate])
+    store([near[1]])
+    store([near[2]])
+    store([near[0], far[0]])
+    store([far[1]])
+    store([far[2]])
     g.sync.wait_ge(S.st, 16 * stores[0])
     g.wait_ge(S.ls, sent[0])

from concourse.bass import DstId, RemoteDMATransfer
from concourse.mybir import dt, AluOpType, ActivationFunctionType

N = 8
WORLD = 256
NC = 128
G = 4
C = 0.00048828125

SCRATCH = {
    "xb": ("sbuf", [128, 4 * NC], "bfloat16"),
    "ub": ("sbuf", [128, G * 512], "bfloat16"),
    "vb": ("sbuf", [128, G * 512], "bfloat16"),
    "wb": ("sbuf", [128, 512], "bfloat16"),
    "xq": ("sbuf", [128, NC], "float8_e4m3fn_x4"),
    "xs": ("sbuf", [128, NC], "uint8"),
    "uq": ("sbuf", [128, G * 128], "float8_e4m3fn_x4"),
    "us": ("sbuf", [128, G * 128], "uint8"),
    "vq": ("sbuf", [128, G * 128], "float8_e4m3fn_x4"),
    "vs": ("sbuf", [128, G * 128], "uint8"),
    "wq": ("sbuf", [128, 128], "float8_e4m3fn_x4"),
    "ws": ("sbuf", [128, 128], "uint8"),
    "rl": ("sbuf", [128, G * NC], "float32"),
    "hb": ("sbuf", [128, 4 * NC], "bfloat16"),
    "hq": ("sbuf", [128, N * NC], "float8_e4m3fn_x4"),
    "hs": ("sbuf", [128, N * NC], "uint8"),
    "yb": ("sbuf", [128, N * NC], "float32"),
    "ps": ("psum", [128, 8 * 512], "float32"),
}
PIECES_U = [(0, 2), (2, 4)]
PIECES_V = [(0, 2), (2, 3), (3, 4)]
SEMAPHORES = (
    ["ld_x", "ld_w", "q_x", "q_w", "q_h", "ml", "ls", "st", "sm", "cm", "fc", "ra", "rb"]
    + ["ld_u%d" % i for i in range(len(PIECES_U))] + ["ld_v%d" % i for i in range(len(PIECES_V))]
    + ["q_u%d" % i for i in range(len(PIECES_U))] + ["q_v%d" % i for i in range(len(PIECES_V))]
    + ["m_u%d" % b for b in range(G)] + ["m_v%d" % b for b in range(G)] + ["r_%d" % b for b in range(G)]
    + ["c%d" % j for j in range(N)] + ["sp%d" % j for j in range(N)]
    + ["cp%d" % j for j in range(N)] + ["my%d" % j for j in range(N)]
)


def rank_program(g, core, T, topo):
    S = T.sem
    cores = list(T.cores)

    def mate_of(c):
        return [d for d in cores if topo.mates(c, d)][0]

    def ring(c):
        plane = [d for d in cores if d == c or topo.same_plane(c, d)]
        me = plane.index(c)
        to = [plane[(me + s) % len(plane)] for s in range(1, len(plane))]
        frm = [plane[(me - s) % len(plane)] for s in range(1, len(plane))]
        return to, frm

    def last_far(c):
        return mate_of(ring(c)[0][-1])

    def passer_of(c):
        return [d for d in range(WORLD) if topo.host(d) == topo.host(c) and topo.chip(d) == topo.chip(c)
                and d not in cores and topo.die(d) != topo.die(c) and topo.may_write(d, last_far(c))][0]

    def masks(c):
        off = topo.mask(c, mate_of(c))
        for d in ring(c)[0]:
            off &= topo.mask(c, d)
        return off, topo.mask(c, passer_of(c)) & ~off

    def count(m):
        return bin(m).count("1")

    def codes(j, n=1):
        return T.hq[:, NC * j:NC * (j + n)].bitcast(dt.uint8)

    def planes(j, n=1):
        return T.hs[:, NC * j:NC * (j + n)]

    sent = [0]

    def send(src, dests, views, sem, mask):
        ids = [DstId(rid=topo.addr(d, core)[0], pnc=topo.addr(d, core)[1]) for d in dests]
        g.remote_dma_fused([RemoteDMATransfer(dst_ids=ids, dma_engine_mask=mask, remote_sem=sem,
                                              srcs=[src], dsts=views)], local_sem=S.ls)
        sent[0] += count(mask)

    OWN, MATE, NEAR, FAR = 0, 1, 2, 5

    rank = T.rank_of(core)
    if rank is None:
        for c in cores:
            if passer_of(c) == core:
                g.wait_ge(S.fc, count(masks(c)[1]))
                send(codes(OWN), [last_far(c)], [codes(FAR + 2)], S.cm, topo.mask(core, last_far(c)))
                g.wait_ge(S.ls, sent[0])
        return

    V, P, A = g.vector, g.tensor, g.scalar
    mate = mate_of(core)
    send_to, near = ring(core)
    far = [mate_of(d) for d in near]
    passer = passer_of(core)
    off, on = masks(core)
    ne = count(off)
    npass = count(topo.mask(passer_of(far[2]), core))
    R = T.rank_of

    def bank(j):
        return T.ps[:, 512 * j:512 * j + NC]

    A.dma_start(T.xb[:], T.x[:]).then_inc(S.ld_x, 16)
    for i, (a, b) in enumerate(PIECES_U):
        g.sync.dma_start(T.ub[:, 512 * a:512 * b], T.u[:, 512 * a:512 * b]).then_inc(S["ld_u%d" % i], 16)
    for i, (a, b) in enumerate(PIECES_V):
        g.sync.dma_start(T.vb[:, 512 * a:512 * b], T.v[:, 512 * a:512 * b]).then_inc(S["ld_v%d" % i], 16)
    g.sync.dma_start(T.wb[:], T.w2[:]).then_inc(S.ld_w, 16)

    def quant(name, i, a, b):
        V.wait_ge(S["ld_%s%d" % (name, i)], 16)
        V.quantize_mx(T[name + "q"][:, 128 * a:128 * b], T[name + "s"][:, 128 * a:128 * b],
                      T[name + "b"][:, 512 * a:512 * b]).then_inc(S["q_%s%d" % (name, i)], 1)

    def gate(b):
        V.wait_ge(S["r_%d" % b], 1)
        V.wait_ge(S["m_v%d" % b], 1)
        V.tensor_tensor(T.hb[:, b:4 * NC:4], T.rl[:, NC * b:NC * b + NC], bank(G + b), AluOpType.mult).then_inc(S.ml, 1)

    V.wait_ge(S.ld_x, 16)
    V.quantize_mx(T.xq[:], T.xs[:], T.xb[:]).then_inc(S.q_x, 1)
    for i, (a, b) in enumerate(PIECES_U):
        quant("u", i, a, b)
    due = []
    for i, (a, b) in enumerate(PIECES_V):
        quant("v", i, a, b)
        for t in due:
            gate(t)
        due = list(range(a, b))
    for t in due:
        gate(t)
    V.wait_ge(S.ml, G)
    V.quantize_mx(T.hq[:, NC * OWN:NC * OWN + NC], planes(0), T.hb[:]).then_inc(S.q_h, 1)
    V.wait_ge(S.ld_w, 16)
    V.quantize_mx(T.wq[:], T.ws[:], T.wb[:]).then_inc(S.q_w, 1)

    P.wait_ge(S.q_x, 1)
    for name, pieces, first in (("u", PIECES_U, 0), ("v", PIECES_V, G)):
        for i, (a, b) in enumerate(pieces):
            P.wait_ge(S["q_%s%d" % (name, i)], 1)
            for t in range(a, b):
                P.matmul_mx(bank(first + t), T[name + "q"][:, 128 * t:128 * t + 128], T[name + "s"][:, 128 * t:128 * t + 128],
                            T.xq[:], T.xs[:], True, True).then_inc(S["m_%s%d" % (name, t)], 1)

    for b in range(G):
        A.wait_ge(S["m_u%d" % b], 1)
        A.activation(T.rl[:, NC * b:NC * b + NC], bank(b), ActivationFunctionType.Relu, scale=C).then_inc(S["r_%d" % b], 1)

    ks = range(len(send_to))
    g.wait_ge(S.q_h, 1)
    send(planes(0), [mate], [planes(1)], S.sm, off)
    send(codes(OWN), send_to + [mate], [codes(NEAR + k) for k in ks] + [codes(MATE)], S["c%d" % rank], off)
    send(codes(OWN), [passer], [codes(OWN)], S.fc, on)
    g.wait_ge(S.sm, ne)
    send(planes(0, 2), send_to, [planes(2 + 2 * k, 2) for k in ks], S["sp%d" % rank], off)
    g.wait_ge(S["c%d" % R(near[0])], ne)
    send(codes(NEAR), [mate], [codes(FAR)], S.ra, off)
    g.wait_ge(S["c%d" % R(near[1])], ne)
    send(codes(NEAR + 1), [mate], [codes(FAR + 1)], S.rb, off)

    todo = [(core, OWN, 0, []), (mate, MATE, 1, [(S.sm, ne), (S["c%d" % R(mate)], ne)])]
    for k, d in enumerate(near):
        todo.append((d, NEAR + k, 2 + 2 * k, [(S["sp%d" % R(d)], ne), (S["c%d" % R(d)], ne)]))
    todo.append((far[0], FAR, 3, [(S.ra, ne)]))
    todo.append((far[1], FAR + 1, 5, [(S.rb, ne)]))
    todo.append((far[2], FAR + 2, 7, [(S.cm, npass)]))
    P.wait_ge(S.q_w, 1)
    P.wait_ge(S.q_h, 1)
    for n, (d, cj, pj, waits) in enumerate(todo):
        r = R(d)
        for sem, val in waits:
            P.wait_ge(sem, val)
        P.matmul_mx(bank(cj), T.wq[:], T.ws[:], T.hq[:, NC * cj:NC * cj + NC], planes(pj), True, True).then_inc(S["my%d" % r], 1)
        if n % 2 == 0:
            V.wait_ge(S["my%d" % r], 1)
            V.tensor_copy(T.yb[:, NC * r:NC * r + NC], bank(cj)).then_inc(S["cp%d" % r], 1)
        else:
            A.wait_ge(S["my%d" % r], 1)
            A.activation(T.yb[:, NC * r:NC * r + NC], bank(cj), ActivationFunctionType.Copy).then_inc(S["cp%d" % r], 1)

    stores = [0]

    def store(ds):
        rs = sorted(R(d) for d in ds)
        for r in rs:
            g.sync.wait_ge(S["cp%d" % r], 1)
        runs = [(rs[0], 2)] if len(rs) == 2 and rs[1] == rs[0] + 1 else [(r, 1) for r in rs]
        for r, w in runs:
            g.sync.dma_start(T.y[:, NC * r:NC * (r + w)], T.yb[:, NC * r:NC * (r + w)]).then_inc(S.st, 16)
            stores[0] += 1

    store([core])
    store([mate])
    store([near[1]])
    store([near[2]])
    store([near[0], far[0]])
    store([far[1]])
    store([far[2]])
    g.sync.wait_ge(S.st, 16 * stores[0])
    g.wait_ge(S.ls, sent[0])
